import numpy as np
import ml_dtypes


def mxq(x, axis, fmt="e4m3"):
    dtype, down = {"e4m3": (ml_dtypes.float8_e4m3fn, 7), "e5m2": (ml_dtypes.float8_e5m2, 14)}[fmt]
    v = np.moveaxis(np.asarray(x, np.float32).astype(ml_dtypes.bfloat16).astype(np.float64), axis, -1)
    blocks = v.reshape(v.shape[:-1] + (-1, 32))
    amax = np.abs(blocks).max(-1, keepdims=True)
    byte = np.maximum(np.where(amax > 0, np.frexp(amax)[1] - 1 + 127, 0) - down, 1)
    scale = np.exp2(byte - 127.0)
    codes = (blocks / scale).astype(np.float32).astype(dtype).astype(np.float64)
    return np.moveaxis((codes * scale).reshape(v.shape), -1, axis)


WIDE = False


def mx_kscale(k):
    if not WIDE:
        return np.ones(k)
    levels = np.array([10, -10, 5, -5, 0])
    if k % 512:
        return np.exp2(np.random.permutation(np.resize(levels, k // 32))).repeat(32)
    a = np.empty((k // 512, 16))
    for p in range(k // 512):
        a[p, :8] = np.random.permutation(np.resize(levels, 8))
        for g in range(8):
            far = levels[np.abs(levels - a[p, g]) >= 10]
            a[p, g + 8] = far[np.random.randint(len(far))]
    return np.exp2(a.ravel()).repeat(32)


def f64(x):
    return np.asarray(x).astype(np.float64)


def striped(idx):
    return np.tile(idx.reshape(-1, 16).T, (8, 1)).astype(np.uint16)


def unstriped(offs):
    return offs[:16].T.reshape(-1).astype(np.int64)


def pack_weight(w):
    k, n = w.shape
    w = f64(np.asarray(w, np.float32).astype(ml_dtypes.bfloat16)).reshape(k // 32, 32, n)
    amax = np.abs(w).max(1)
    byte = np.clip(np.where(amax > 0, np.frexp(amax)[1] - 1 + 127 - 7, 1), 1, 254)
    scaled = (w * np.exp2(127.0 - byte)[:, None, :]).reshape(k, n).astype(np.float32)
    words = np.ascontiguousarray(scaled.reshape(k // 512, 128, 4, n).transpose(0, 1, 3, 2)).astype(ml_dtypes.float8_e4m3fn).view(np.uint8)
    return words, np.ascontiguousarray(byte.astype(np.uint8).reshape(k // 512, 16, n))


def unpack_weight(words, scales):
    g, p, n, _ = words.shape
    vals = np.ascontiguousarray(words).view(ml_dtypes.float8_e4m3fn).astype(np.float64) * np.repeat(np.exp2(scales.astype(np.float64) - 127.0), 8, axis=1)[..., None]
    return vals.transpose(0, 1, 3, 2).reshape(g * 512, n)


K, T, S, D, N, V = 1024, 2048, 1024, 8, 128, 128
P = 2 ** 7


def setup_inputs():
    n = np.random.standard_normal
    s = mx_kscale(K)[:, None]
    packed_xT = pack_weight(n((K, T)) * s)
    return {
        "x_words": packed_xT[0],
        "x_scales": packed_xT[1],
        "w1": (n((K, N)) / np.sqrt(K) / s).astype(np.float32),
        "w2": (n((K, N)) / np.sqrt(K) / s).astype(np.float32),
        "alpha": (np.tile(np.random.uniform(0.65, 0.75, V) * D * D, (P, 1))).astype(np.float32),
        "offs": striped(np.random.permutation(T)[:S]),
    }


def reference(x_words, x_scales, w1, w2, alpha, offs):
    xq = unpack_weight(x_words, x_scales)[:, unstriped(offs)]
    y = mxq(f64(w1), 0, "e4m3").T @ xq
    z = mxq(f64(w2), 0, "e4m3").T @ xq
    reg = np.maximum(np.log(np.exp(y) + 1.0), np.log(np.exp(z) + 1.0))
    inv = np.exp(-0.693147 * reg)
    tot = inv.reshape(len(inv), -1, D).sum(axis=2)
    est = f64(alpha)[:1] / tot
    return np.log(est)

@@ -1,0 +1,185 @@
+import math
+from contextlib import ExitStack
+
+import concourse.mybir as mybir
+
+K, T, S, D, N, V = 1024, 2048, 1024, 8, 128, 128
+P = 128
+PACK = 4
+K_PASS = P * PACK
+PASSES = K // K_PASS
+CHUNK = 256
+CHUNKS = S // CHUNK
+C = 0.693147
+SHIFT = 64
+
+FLOPS = 2 * 2 * K * N * S
+
+F32 = mybir.dt.float32
+BF16 = mybir.dt.bfloat16
+I32 = mybir.dt.int32
+U32 = mybir.dt.uint32
+U16 = mybir.dt.uint16
+U8 = mybir.dt.uint8
+FP8X4 = mybir.dt.float8_e4m3fn_x4
+ACT = mybir.ActivationFunctionType
+ALU = mybir.AluOpType
+AX = mybir.AxisListType
+
+
+def tile_picked_yhll_est_p_kernel(tc, x_words, x_scales, w1, w2, alpha, offs, out):
+    nc = tc.nc
+    with ExitStack() as ctx:
+        keep = ctx.enter_context(tc.tile_pool(name="keep", bufs=1))
+        psum = ctx.enter_context(tc.psum_pool(name="psum", bufs=1))
+
+        offsets = keep.tile([P, S // 16], U16, name="offsets")
+        nc.sync.dma_start(offsets[:], offs)
+
+        scale_table = keep.tile([P, T], U8, name="scale_table", align_bytes=64)
+        nc.vector.memset(scale_table[:].bitcast(I32), 0)
+        for q in range(4):
+            nc.sync.dma_start(
+                out=scale_table[32 * q : 32 * q + 4 * PASSES, :].bitcast(I32),
+                in_=x_scales[:, 4 * q : 4 * q + 4, :].bitcast(I32),
+            )
+
+        word_table = [keep.tile([P, T], U32, name="word_table%d" % g, align_bytes=64) for g in range(PASSES)]
+
+        def load_words(g):
+            nc.sync.dma_start(
+                out=word_table[g][:].bitcast(I32),
+                in_=x_words[g].rearrange("p c r -> p (c r)").bitcast(I32),
+            )
+
+        w_raw = {}
+
+        def load_weights(i, w, g0, g1):
+            raw = keep.tile([P, g1 - g0, PACK, N], F32, name="w_raw%d_%d" % (i, g0))
+            nc.sync.dma_start(
+                out=raw[:],
+                in_=w[g0 * K_PASS : g1 * K_PASS, :].rearrange("(g p j) m -> p g j m", g=g1 - g0, j=PACK),
+            )
+            for g in range(g0, g1):
+                w_raw[i, g] = raw[:, g - g0]
+
+        load_weights(0, w1, 0, 2)
+        load_words(0)
+        load_weights(1, w2, 0, 1)
+        load_words(1)
+        load_weights(1, w2, 1, 2)
+        tail_in = keep.tile([P, 2 * V], F32, name="tail_in")
+        nc.sync.dma_start(out=tail_in[:, 0:V], in_=alpha)
+
+        tiny = keep.tile([P, 1], F32, name="tiny")
+        nc.gpsimd.memset(tiny[:], 2.0**-SHIFT)
+
+        picked_scales = keep.tile([P, S], U8, name="picked_scales", align_bytes=64)
+        nc.vector.tensor_copy(picked_scales[:], scale_table[:].indirect(offsets[:]))
+
+        w_codes, w_scales = {}, {}
+
+        def quantise_weights(i, g0, g1):
+            n = g1 - g0
+            grouped = keep.tile([P, n, N, PACK], BF16, name="grouped%d_%d" % (i, g0), align_bytes=64)
+            for g in range(g0, g1):
+                nc.scalar.copy(out=grouped[:, g - g0], in_=w_raw[i, g].rearrange("p j m -> p m j"))
+            codes = keep.tile([P, n * N], U32, name="w_codes%d_%d" % (i, g0), align_bytes=64)
+            scales = keep.tile([P, n * N], U8, name="w_scales%d_%d" % (i, g0), align_bytes=64)
+            nc.vector.quantize_mx(
+                out=codes[:].bitcast(FP8X4),
+                scales=scales[:],
+                in_=grouped[:].rearrange("p g m j -> p (g m j)"),
+            )
+            for g in range(g0, g1):
+                w_codes[i, g] = codes[:, (g - g0) * N : (g - g0 + 1) * N]
+                w_scales[i, g] = scales[:, (g - g0) * N : (g - g0 + 1) * N]
+
+        quantise_weights(0, 0, 2)
+        picked0 = keep.tile([P, S], U32, name="picked0", align_bytes=64)
+        for h in range(2):
+            nc.vector.tensor_copy(
+                picked0[:, h * S // 2 : (h + 1) * S // 2],
+                word_table[0][:].indirect(offsets[:, h * S // 32 : (h + 1) * S // 32]),
+            )
+        quantise_weights(1, 0, 1)
+
+        acc = {}
+        for c in range(CHUNKS):
+            for i in range(2):
+                acc[c, i] = psum.tile([P, CHUNK], F32, name="acc%d_%d" % (c, i))
+
+        def product(c, i, g, words):
+            cols = slice(c * CHUNK, (c + 1) * CHUNK)
+            nc.tensor.matmul_mx(
+                out=acc[c, i][:],
+                lhsT=w_codes[i, g].bitcast(FP8X4),
+                lhsT_scale=w_scales[i, g],
+                rhs=words.bitcast(FP8X4),
+                rhs_scale=picked_scales[4 * g : P, cols],
+                start=(g == 0),
+                stop=(g == PASSES - 1),
+            )
+
+        for i in range(2):
+            for c in range(CHUNKS):
+                product(c, i, 0, picked0[:, c * CHUNK : (c + 1) * CHUNK])
+
+        expo = keep.tile([P, 2, S], F32, name="expo")
+        picked1 = {}
+
+        def gather_last(c):
+            picked1[c] = keep.tile([P, CHUNK], U32, name="picked1_%d" % c, align_bytes=64)
+            nc.vector.tensor_copy(
+                picked1[c][:], word_table[1][:].indirect(offsets[:, c * CHUNK // 16 : (c + 1) * CHUNK // 16])
+            )
+
+        def finish(c, i):
+            product(c, i, 1, picked1[c][:])
+            nc.scalar.activation(out=expo[:, i, c * CHUNK : (c + 1) * CHUNK], in_=acc[c, i][:], func=ACT.Exp)
+
+        for c in range(2):
+            gather_last(c)
+        quantise_weights(1, 1, 2)
+        for c in range(2):
+            finish(c, 0)
+        for c in range(2):
+            finish(c, 1)
+        for c in range(2, CHUNKS):
+            gather_last(c)
+            for i in range(2):
+                finish(c, i)
+
+        LATE = 32
+        MAIN = S - LATE
+        larger = keep.tile([P, MAIN], F32, name="larger")
+        reg = keep.tile([P, S], F32, name="reg")
+        both = keep.tile([P, 2, LATE], F32, name="both")
+        nc.scalar.activation(out=both[:], in_=expo[:, :, MAIN:S], func=ACT.Ln, scale=2.0**-SHIFT, bias=tiny[:])
+        nc.vector.tensor_tensor(out=larger[:], in0=expo[:, 0, 0:MAIN], in1=expo[:, 1, 0:MAIN], op=ALU.max)
+        nc.vector.tensor_tensor(out=reg[:, MAIN:S], in0=both[:, 0, :], in1=both[:, 1, :], op=ALU.max)
+        nc.scalar.activation(out=reg[:, 0:MAIN], in_=larger[:], func=ACT.Ln, scale=2.0**-SHIFT, bias=tiny[:])
+        inv = keep.tile([P, S], F32, name="inv")
+        EARLY = 48
+        for v0, v1 in ((0, EARLY), (EARLY, V)):
+            cols = slice(v0 * D, v1 * D)
+            nc.scalar.activation(out=inv[:, cols], in_=reg[:, cols], func=ACT.Exp, scale=-C)
+            nc.vector.tensor_reduce(
+                out=tail_in[:, V + v0 : V + v1],
+                in_=inv[:, cols].rearrange("p (v d) -> p v d", d=D),
+                axis=AX.X,
+                op=ALU.add,
+            )
+        logs = keep.tile([P, 2 * V], F32, name="logs")
+        for cols in (slice(0, V + EARLY), slice(V + EARLY, 2 * V)):
+            nc.scalar.activation(out=logs[:, cols], in_=tail_in[:, cols], func=ACT.Ln)
+        result = keep.tile([P, V], F32, name="result")
+        nc.vector.scalar_tensor_tensor(
+            out=result[:],
+            in0=logs[:, 0:V],
+            scalar=C * SHIFT * math.log(2.0),
+            in1=logs[:, V : 2 * V],
+            op0=ALU.add,
+            op1=ALU.subtract,
+        )
+        nc.sync.dma_start(out=out, in_=result[:])

@@ -12,6 +12,9 @@ CHUNK = 256
 CHUNKS = S // CHUNK
 C = 0.693147
 SHIFT = 64
+LATE = 32
+MAIN = S - LATE
+EARLY = 32
 
 FLOPS = 2 * 2 * K * N * S
 
@@ -63,8 +66,9 @@ def tile_picked_yhll_est_p_kernel(tc, x_words, x_scales, w1, w2, alpha, offs, ou
             for g in range(g0, g1):
                 w_raw[i, g] = raw[:, g - g0]
 
-        load_weights(0, w1, 0, 2)
+        load_weights(0, w1, 0, 1)
         load_words(0)
+        load_weights(0, w1, 1, 2)
         load_weights(1, w2, 0, 1)
         load_words(1)
         load_weights(1, w2, 1, 2)
@@ -81,7 +85,7 @@ def tile_picked_yhll_est_p_kernel(tc, x_words, x_scales, w1, w2, alpha, offs, ou
 
         def quantise_weights(i, g0, g1):
             n = g1 - g0
-            grouped = keep.tile([P, n, N, PACK], BF16, name="grouped%d_%d" % (i, g0), align_bytes=64)
+            grouped = keep.tile([P, n, N, PACK], BF16, name="grouped%d_%d" % (i, g0), tag="reused%d_%d" % (i, g0), align_bytes=64)
             for g in range(g0, g1):
                 nc.scalar.copy(out=grouped[:, g - g0], in_=w_raw[i, g].rearrange("p j m -> p m j"))
             codes = keep.tile([P, n * N], U32, name="w_codes%d_%d" % (i, g0), align_bytes=64)
@@ -95,7 +99,7 @@ def tile_picked_yhll_est_p_kernel(tc, x_words, x_scales, w1, w2, alpha, offs, ou
                 w_codes[i, g] = codes[:, (g - g0) * N : (g - g0 + 1) * N]
                 w_scales[i, g] = scales[:, (g - g0) * N : (g - g0 + 1) * N]
 
-        quantise_weights(0, 0, 2)
+        quantise_weights(0, 0, 1)
         picked0 = keep.tile([P, S], U32, name="picked0", align_bytes=64)
         for h in range(2):
             nc.vector.tensor_copy(
@@ -103,6 +107,7 @@ def tile_picked_yhll_est_p_kernel(tc, x_words, x_scales, w1, w2, alpha, offs, ou
                 word_table[0][:].indirect(offsets[:, h * S // 32 : (h + 1) * S // 32]),
             )
         quantise_weights(1, 0, 1)
+        quantise_weights(0, 1, 2)
 
         acc = {}
         for c in range(CHUNKS):
@@ -128,39 +133,41 @@ def tile_picked_yhll_est_p_kernel(tc, x_words, x_scales, w1, w2, alpha, offs, ou
         expo = keep.tile([P, 2, S], F32, name="expo")
         picked1 = {}
 
-        def gather_last(c):
-            picked1[c] = keep.tile([P, CHUNK], U32, name="picked1_%d" % c, align_bytes=64)
-            nc.vector.tensor_copy(
-                picked1[c][:], word_table[1][:].indirect(offsets[:, c * CHUNK // 16 : (c + 1) * CHUNK // 16])
-            )
+        def gather_last(half, tag):
+            words = keep.tile([P, S // 2], U32, name="picked1_%d" % half, tag=tag, align_bytes=64)
+            for c in (2 * half, 2 * half + 1):
+                picked1[c] = words[:, (c % 2) * CHUNK : (c % 2 + 1) * CHUNK]
+                nc.vector.tensor_copy(
+                    picked1[c], word_table[1][:].indirect(offsets[:, c * CHUNK // 16 : (c + 1) * CHUNK // 16])
+                )
 
         def finish(c, i):
-            product(c, i, 1, picked1[c][:])
-            nc.scalar.activation(out=expo[:, i, c * CHUNK : (c + 1) * CHUNK], in_=acc[c, i][:], func=ACT.Exp)
+            product(c, i, 1, picked1[c])
+            spans = ((CHUNK - LATE, CHUNK), (0, CHUNK - LATE)) if (c, i) == (CHUNKS - 1, 1) else ((0, CHUNK),)
+            for lo, hi in spans:
+                nc.scalar.activation(
+                    out=expo[:, i, c * CHUNK + lo : c * CHUNK + hi], in_=acc[c, i][:, lo:hi], func=ACT.Exp
+                )
 
-        for c in range(2):
-            gather_last(c)
+        gather_last(0, "reused0_1")
         quantise_weights(1, 1, 2)
-        for c in range(2):
-            finish(c, 0)
-        for c in range(2):
-            finish(c, 1)
+        for i in range(2):
+            for c in range(2):
+                finish(c, i)
+        gather_last(1, "reused1_1")
         for c in range(2, CHUNKS):
-            gather_last(c)
             for i in range(2):
                 finish(c, i)
 
-        LATE = 32
-        MAIN = S - LATE
         larger = keep.tile([P, MAIN], F32, name="larger")
         reg = keep.tile([P, S], F32, name="reg")
         both = keep.tile([P, 2, LATE], F32, name="both")
         nc.scalar.activation(out=both[:], in_=expo[:, :, MAIN:S], func=ACT.Ln, scale=2.0**-SHIFT, bias=tiny[:])
         nc.vector.tensor_tensor(out=larger[:], in0=expo[:, 0, 0:MAIN], in1=expo[:, 1, 0:MAIN], op=ALU.max)
         nc.vector.tensor_tensor(out=reg[:, MAIN:S], in0=both[:, 0, :], in1=both[:, 1, :], op=ALU.max)
-        nc.scalar.activation(out=reg[:, 0:MAIN], in_=larger[:], func=ACT.Ln, scale=2.0**-SHIFT, bias=tiny[:])
+        for cols in (slice(0, EARLY * D), slice(EARLY * D, MAIN)):
+            nc.scalar.activation(out=reg[:, cols], in_=larger[:, cols], func=ACT.Ln, scale=2.0**-SHIFT, bias=tiny[:])
         inv = keep.tile([P, S], F32, name="inv")
-        EARLY = 48
         for v0, v1 in ((0, EARLY), (EARLY, V)):
             cols = slice(v0 * D, v1 * D)
             nc.scalar.activation(out=inv[:, cols], in_=reg[:, cols], func=ACT.Exp, scale=-C)

@@ -87,7 +87,10 @@ def tile_picked_yhll_est_p_kernel(tc, x_words, x_scales, w1, w2, alpha, offs, ou
             n = g1 - g0
             grouped = keep.tile([P, n, N, PACK], BF16, name="grouped%d_%d" % (i, g0), tag="reused%d_%d" % (i, g0), align_bytes=64)
             for g in range(g0, g1):
-                nc.scalar.copy(out=grouped[:, g - g0], in_=w_raw[i, g].rearrange("p j m -> p m j"))
+                nc.scalar.copy(
+                    out=grouped[:, g - g0].rearrange("p (c i) j -> p c j i", i=4),
+                    in_=w_raw[i, g].rearrange("p j (c i) -> p c j i", i=4),
+                )
             codes = keep.tile([P, n * N], U32, name="w_codes%d_%d" % (i, g0), align_bytes=64)
             scales = keep.tile([P, n * N], U8, name="w_scales%d_%d" % (i, g0), align_bytes=64)
             nc.vector.quantize_mx(

import math
from contextlib import ExitStack

import concourse.mybir as mybir

K, T, S, D, N, V = 1024, 2048, 1024, 8, 128, 128
P = 128
PACK = 4
K_PASS = P * PACK
PASSES = K // K_PASS
CHUNK = 256
CHUNKS = S // CHUNK
C = 0.693147
SHIFT = 64
LATE = 32
MAIN = S - LATE
EARLY = 32

FLOPS = 2 * 2 * K * N * S

F32 = mybir.dt.float32
BF16 = mybir.dt.bfloat16
I32 = mybir.dt.int32
U32 = mybir.dt.uint32
U16 = mybir.dt.uint16
U8 = mybir.dt.uint8
FP8X4 = mybir.dt.float8_e4m3fn_x4
ACT = mybir.ActivationFunctionType
ALU = mybir.AluOpType
AX = mybir.AxisListType


def tile_picked_yhll_est_p_kernel(tc, x_words, x_scales, w1, w2, alpha, offs, out):
    nc = tc.nc
    with ExitStack() as ctx:
        keep = ctx.enter_context(tc.tile_pool(name="keep", bufs=1))
        psum = ctx.enter_context(tc.psum_pool(name="psum", bufs=1))

        offsets = keep.tile([P, S // 16], U16, name="offsets")
        nc.sync.dma_start(offsets[:], offs)

        scale_table = keep.tile([P, T], U8, name="scale_table", align_bytes=64)
        nc.vector.memset(scale_table[:].bitcast(I32), 0)
        for q in range(4):
            nc.sync.dma_start(
                out=scale_table[32 * q : 32 * q + 4 * PASSES, :].bitcast(I32),
                in_=x_scales[:, 4 * q : 4 * q + 4, :].bitcast(I32),
            )

        word_table = [keep.tile([P, T], U32, name="word_table%d" % g, align_bytes=64) for g in range(PASSES)]

        def load_words(g):
            nc.sync.dma_start(
                out=word_table[g][:].bitcast(I32),
                in_=x_words[g].rearrange("p c r -> p (c r)").bitcast(I32),
            )

        w_raw = {}

        def load_weights(i, w, g0, g1):
            raw = keep.tile([P, g1 - g0, PACK, N], F32, name="w_raw%d_%d" % (i, g0))
            nc.sync.dma_start(
                out=raw[:],
                in_=w[g0 * K_PASS : g1 * K_PASS, :].rearrange("(g p j) m -> p g j m", g=g1 - g0, j=PACK),
            )
            for g in range(g0, g1):
                w_raw[i, g] = raw[:, g - g0]

        load_weights(0, w1, 0, 1)
        load_words(0)
        load_weights(0, w1, 1, 2)
        load_weights(1, w2, 0, 1)
        load_words(1)
        load_weights(1, w2, 1, 2)
        tail_in = keep.tile([P, 2 * V], F32, name="tail_in")
        nc.sync.dma_start(out=tail_in[:, 0:V], in_=alpha)

        tiny = keep.tile([P, 1], F32, name="tiny")
        nc.gpsimd.memset(tiny[:], 2.0**-SHIFT)

        picked_scales = keep.tile([P, S], U8, name="picked_scales", align_bytes=64)
        nc.vector.tensor_copy(picked_scales[:], scale_table[:].indirect(offsets[:]))

        w_codes, w_scales = {}, {}

        def quantise_weights(i, g0, g1):
            n = g1 - g0
            grouped = keep.tile([P, n, N, PACK], BF16, name="grouped%d_%d" % (i, g0), tag="reused%d_%d" % (i, g0), align_bytes=64)
            for g in range(g0, g1):
                nc.scalar.copy(
                    out=grouped[:, g - g0].rearrange("p (c i) j -> p c j i", i=4),
                    in_=w_raw[i, g].rearrange("p j (c i) -> p c j i", i=4),
                )
            codes = keep.tile([P, n * N], U32, name="w_codes%d_%d" % (i, g0), align_bytes=64)
            scales = keep.tile([P, n * N], U8, name="w_scales%d_%d" % (i, g0), align_bytes=64)
            nc.vector.quantize_mx(
                out=codes[:].bitcast(FP8X4),
                scales=scales[:],
                in_=grouped[:].rearrange("p g m j -> p (g m j)"),
            )
            for g in range(g0, g1):
                w_codes[i, g] = codes[:, (g - g0) * N : (g - g0 + 1) * N]
                w_scales[i, g] = scales[:, (g - g0) * N : (g - g0 + 1) * N]

        quantise_weights(0, 0, 1)
        picked0 = keep.tile([P, S], U32, name="picked0", align_bytes=64)
        for h in range(2):
            nc.vector.tensor_copy(
                picked0[:, h * S // 2 : (h + 1) * S // 2],
                word_table[0][:].indirect(offsets[:, h * S // 32 : (h + 1) * S // 32]),
            )
        quantise_weights(1, 0, 1)
        quantise_weights(0, 1, 2)

        acc = {}
        for c in range(CHUNKS):
            for i in range(2):
                acc[c, i] = psum.tile([P, CHUNK], F32, name="acc%d_%d" % (c, i))

        def product(c, i, g, words):
            cols = slice(c * CHUNK, (c + 1) * CHUNK)
            nc.tensor.matmul_mx(
                out=acc[c, i][:],
                lhsT=w_codes[i, g].bitcast(FP8X4),
                lhsT_scale=w_scales[i, g],
                rhs=words.bitcast(FP8X4),
                rhs_scale=picked_scales[4 * g : P, cols],
                start=(g == 0),
                stop=(g == PASSES - 1),
            )

        for i in range(2):
            for c in range(CHUNKS):
                product(c, i, 0, picked0[:, c * CHUNK : (c + 1) * CHUNK])

        expo = keep.tile([P, 2, S], F32, name="expo")
        picked1 = {}

        def gather_last(half, tag):
            words = keep.tile([P, S // 2], U32, name="picked1_%d" % half, tag=tag, align_bytes=64)
            for c in (2 * half, 2 * half + 1):
                picked1[c] = words[:, (c % 2) * CHUNK : (c % 2 + 1) * CHUNK]
                nc.vector.tensor_copy(
                    picked1[c], word_table[1][:].indirect(offsets[:, c * CHUNK // 16 : (c + 1) * CHUNK // 16])
                )

        def finish(c, i):
            product(c, i, 1, picked1[c])
            spans = ((CHUNK - LATE, CHUNK), (0, CHUNK - LATE)) if (c, i) == (CHUNKS - 1, 1) else ((0, CHUNK),)
            for lo, hi in spans:
                nc.scalar.activation(
                    out=expo[:, i, c * CHUNK + lo : c * CHUNK + hi], in_=acc[c, i][:, lo:hi], func=ACT.Exp
                )

        gather_last(0, "reused0_1")
        quantise_weights(1, 1, 2)
        for i in range(2):
            for c in range(2):
                finish(c, i)
        gather_last(1, "reused1_1")
        for c in range(2, CHUNKS):
            for i in range(2):
                finish(c, i)

        larger = keep.tile([P, MAIN], F32, name="larger")
        reg = keep.tile([P, S], F32, name="reg")
        both = keep.tile([P, 2, LATE], F32, name="both")
        nc.scalar.activation(out=both[:], in_=expo[:, :, MAIN:S], func=ACT.Ln, scale=2.0**-SHIFT, bias=tiny[:])
        nc.vector.tensor_tensor(out=larger[:], in0=expo[:, 0, 0:MAIN], in1=expo[:, 1, 0:MAIN], op=ALU.max)
        nc.vector.tensor_tensor(out=reg[:, MAIN:S], in0=both[:, 0, :], in1=both[:, 1, :], op=ALU.max)
        for cols in (slice(0, EARLY * D), slice(EARLY * D, MAIN)):
            nc.scalar.activation(out=reg[:, cols], in_=larger[:, cols], func=ACT.Ln, scale=2.0**-SHIFT, bias=tiny[:])
        inv = keep.tile([P, S], F32, name="inv")
        for v0, v1 in ((0, EARLY), (EARLY, V)):
            cols = slice(v0 * D, v1 * D)
            nc.scalar.activation(out=inv[:, cols], in_=reg[:, cols], func=ACT.Exp, scale=-C)
            nc.vector.tensor_reduce(
                out=tail_in[:, V + v0 : V + v1],
                in_=inv[:, cols].rearrange("p (v d) -> p v d", d=D),
                axis=AX.X,
                op=ALU.add,
            )
        logs = keep.tile([P, 2 * V], F32, name="logs")
        for cols in (slice(0, V + EARLY), slice(V + EARLY, 2 * V)):
            nc.scalar.activation(out=logs[:, cols], in_=tail_in[:, cols], func=ACT.Ln)
        result = keep.tile([P, V], F32, name="result")
        nc.vector.scalar_tensor_tensor(
            out=result[:],
            in0=logs[:, 0:V],
            scalar=C * SHIFT * math.log(2.0),
            in1=logs[:, V : 2 * V],
            op0=ALU.add,
            op1=ALU.subtract,
        )
        nc.sync.dma_start(out=out, in_=result[:])
